import numpy as np
import ml_dtypes


def mxq(x, axis, fmt="e4m3"):
    dtype, down = {"e4m3": (ml_dtypes.float8_e4m3fn, 7), "e5m2": (ml_dtypes.float8_e5m2, 14)}[fmt]
    v = np.moveaxis(np.asarray(x, np.float32).astype(ml_dtypes.bfloat16).astype(np.float64), axis, -1)
    blocks = v.reshape(v.shape[:-1] + (-1, 32))
    amax = np.abs(blocks).max(-1, keepdims=True)
    byte = np.maximum(np.where(amax > 0, np.frexp(amax)[1] - 1 + 127, 0) - down, 1)
    scale = np.exp2(byte - 127.0)
    codes = (blocks / scale).astype(np.float32).astype(dtype).astype(np.float64)
    return np.moveaxis((codes * scale).reshape(v.shape), -1, axis)


WIDE = False


def mx_kscale(k):
    if not WIDE:
        return np.ones(k)
    levels = np.array([10, -10, 5, -5, 0])
    if k % 512:
        return np.exp2(np.random.permutation(np.resize(levels, k // 32))).repeat(32)
    a = np.empty((k // 512, 16))
    for p in range(k // 512):
        a[p, :8] = np.random.permutation(np.resize(levels, 8))
        for g in range(8):
            far = levels[np.abs(levels - a[p, g]) >= 10]
            a[p, g + 8] = far[np.random.randint(len(far))]
    return np.exp2(a.ravel()).repeat(32)


def f64(x):
    return np.asarray(x).astype(np.float64)


def striped(idx):
    return np.tile(np.asarray(idx).reshape(-1, 16).T, (8, 1)).astype(np.uint16)


def unstriped(offs):
    return offs[:16].T.reshape(-1).astype(np.int64)


E2M1 = np.array([0.0, 0.5, 1.0, 1.5, 2.0, 3.0, 4.0, 6.0, -0.0, -0.5, -1.0, -1.5, -2.0, -3.0, -4.0, -6.0])


def pack_weight(w, fmt):
    k, n = w.shape
    w = f64(np.asarray(w, np.float32).astype(ml_dtypes.bfloat16)).reshape(k // 32, 32, n)
    amax = np.abs(w).max(1)
    if fmt == "e4m3":
        byte = np.frexp(amax)[1] - 1 + 127 - 7
    else:
        mant, ex = np.frexp(amax / 6.0)
        byte = np.where(mant > 0.5, ex, ex - 1) + 127
    byte = np.clip(np.where(amax > 0, byte, 1), 1, 254)
    scaled = (w * np.exp2(127.0 - byte)[:, None, :]).reshape(k, n).astype(np.float32)
    by_word = np.ascontiguousarray(scaled.reshape(k // 512, 128, 4, n).transpose(0, 1, 3, 2))
    if fmt == "e4m3":
        words = by_word.astype(ml_dtypes.float8_e4m3fn).view(np.uint8)
    else:
        c = by_word.astype(ml_dtypes.float4_e2m1fn).view(np.uint8) & 0xF
        words = (c[..., 0::2] | (c[..., 1::2] << 4)).reshape(k // 512, 128, 2 * n)
    return np.ascontiguousarray(words), np.ascontiguousarray(byte.astype(np.uint8).reshape(k // 512, 16, n))


def unpack_weight(words, scales, fmt):
    g, _, n = scales.shape
    words = np.ascontiguousarray(words).reshape(g, 128, n, -1)
    if fmt == "e4m3":
        vals = words.view(ml_dtypes.float8_e4m3fn).astype(np.float64)
    else:
        nib = np.empty((g, 128, n, 4), np.uint8)
        nib[..., 0::2] = words & 0xF
        nib[..., 1::2] = words >> 4
        vals = E2M1[nib]
    vals = vals * np.repeat(np.exp2(scales.astype(np.float64) - 127.0), 8, axis=1)[..., None]
    return vals.transpose(0, 1, 3, 2).reshape(g * 512, n)


B, N, T, D, NQ = 1, 1024, 4096, 512, 128
SEG = 16


def setup_inputs():
    n = np.random.standard_normal
    pages = np.random.permutation(T // 16)[:B * N // 16]
    idx = (pages[:, None] * 16 + np.arange(16)[None, :]).reshape(-1)
    s = mx_kscale(D)[:, None]
    kp = pack_weight(n((D, T)) / s, "e4m3")
    return {
        "qT": (n((B, D, NQ)) * s * (1.00 / np.sqrt(D))).astype(np.float32),
        "k_words": kp[0],
        "k_scales": kp[1],
        "kn": np.tile(np.random.uniform(4.0, 8.0, 4096), (128, 1)).astype(np.float32),
        "qn": (np.random.uniform(4.0, 8.0, (B, NQ, 1))).astype(np.float32),
        "offs": striped(idx),
    }


def reference(qT, k_words, k_scales, kn, qn, offs):
    idx = unstriped(offs)
    pick = lambda x, which: x[:, which].reshape(x.shape[0], B, -1).transpose(1, 0, 2)
    k = unpack_weight(k_words, k_scales, "e4m3")
    kg = pick(k, idx)
    qq = mxq(f64(qT), 1, "e4m3")
    a = qq.transpose(0, 2, 1) @ kg
    y = f64(qn) - (2.0 * a - pick(f64(kn), idx)[:, :1, :]).reshape(B, NQ, N // SEG, SEG).max(-1)
    return y

@@ -1,0 +1,111 @@
+from contextlib import ExitStack
+
+import concourse.mybir as mybir
+from concourse.masks import make_identity
+
+F32 = mybir.dt.float32
+BF16 = mybir.dt.bfloat16
+I32 = mybir.dt.int32
+U32 = mybir.dt.uint32
+U16 = mybir.dt.uint16
+U8 = mybir.dt.uint8
+FP8X4 = mybir.dt.float8_e4m3fn_x4
+ALU = mybir.AluOpType
+ACT = mybir.ActivationFunctionType
+AX = mybir.AxisListType
+
+P = 128
+T = 4096
+N = 1024
+NQ = 128
+D = 512
+SEG = 16
+HALF = 512
+BLOCKS = N // P
+KN_ROW = P - 1
+
+FLOPS = 2 * NQ * N * D
+BYTES = T * D + 16 * T + 4 * T + 4 * D * NQ + 4 * NQ + 2 * N * 8 + 4 * NQ * (N // SEG)
+
+
+def tile_attend_celldist_kernel(tc, qT, k_words, k_scales, kn, qn, offs, out):
+    nc = tc.nc
+    with ExitStack() as ctx:
+        keep = ctx.enter_context(tc.tile_pool(name="keep", bufs=1))
+        psum_a = ctx.enter_context(tc.psum_pool(name="psum_a", bufs=4))
+        psum_t = ctx.enter_context(tc.psum_pool(name="psum_t", bufs=1))
+
+        offsets = keep.tile([P, N // 16], U16, name="offsets")
+        scale_table = keep.tile([P, T], U8, name="scale_table", align_bytes=64)
+        kn_table = keep.tile([P, T], F32, name="kn_table")
+        word_table = keep.tile([P, T], I32, name="word_table")
+        q_raw = keep.tile([P, 4, NQ], F32, name="q_raw")
+        qn_col = keep.tile([P, 1], F32, name="qn_col")
+        ident = keep.tile([P, P], F32, name="ident")
+
+        nc.vector.memset(scale_table[:].bitcast(I32), 0)
+        nc.sync.dma_start(offsets[:], offs)
+        nc.sync.dma_start(out=q_raw[:], in_=qT[0].rearrange("(p j) q -> p j q", j=4))
+        nc.sync.dma_start(out=word_table[:], in_=k_words[0].rearrange("p n t -> p (n t)").bitcast(I32))
+        nc.sync.dma_start(out=qn_col[:], in_=qn[0])
+        nc.scalar.dma_start(out=kn_table[KN_ROW:P, :], in_=kn[0:1, :])
+        for r in range(4):
+            nc.scalar.dma_start(out=scale_table[r:P:32, :].bitcast(I32), in_=k_scales[0][r:16:4, :].bitcast(I32))
+        nc.vector.memset(kn_table[0:KN_ROW, :], 0.0)
+        make_identity(nc, ident[:])
+
+        q_bf = keep.tile([P, NQ, 4], BF16, name="q_bf", align_bytes=64)
+        nc.scalar.copy(out=q_bf[:], in_=q_raw[:].rearrange("p j q -> p q j"))
+
+        kn_g = keep.tile([P, N], F32, name="kn_g")
+        nc.vector.tensor_copy(kn_g[:], kn_table[:].indirect(offsets[:]))
+
+        q_codes = keep.tile([P, NQ], U32, name="q_codes", align_bytes=64)
+        q_scales = keep.tile([P, NQ], U8, name="q_scales", align_bytes=64)
+        nc.vector.quantize_mx(out=q_codes[:].bitcast(FP8X4), scales=q_scales[:], in_=q_bf[:].rearrange("p q j -> p (q j)"))
+
+        scale_g = keep.tile([P, N], U8, name="scale_g", align_bytes=64)
+        nc.vector.tensor_copy(scale_g[:], scale_table[:].indirect(offsets[:]))
+
+        turned = [psum_t.tile([P, 4, P], F32, name=f"turned{i}") for i in range(4)]
+        kn_col = keep.tile([P, BLOCKS], F32, name="kn_col")
+        for h in range(2):
+            for j in range(4):
+                b = 4 * h + j
+                nc.tensor.transpose(turned[h][:, j, :], kn_g[:, b * P:(b + 1) * P], ident[:])
+            nc.scalar.copy(out=kn_col[:, 4 * h:4 * h + 4], in_=turned[h][:, :, KN_ROW])
+
+        word_g = [keep.tile([P, HALF], U32, name=f"word_g{h}", align_bytes=64) for h in range(2)]
+        for h in range(2):
+            nc.vector.tensor_copy(word_g[h][:], word_table[:].bitcast(U32).indirect(offsets[:, 32 * h:32 * (h + 1)]))
+
+        dist = [keep.tile([P, NQ], F32, name=f"dist{b}") for b in range(BLOCKS)]
+        nearest = keep.tile([P, N // SEG], F32, name="nearest")
+
+        def score(b):
+            h, j = divmod(b, 4)
+            a = psum_a.tile([P, NQ], F32, name="a")
+            nc.tensor.matmul_mx(out=a[:], lhsT=word_g[h][:, j * P:(j + 1) * P].bitcast(FP8X4),
+                                lhsT_scale=scale_g[:, b * P:(b + 1) * P],
+                                rhs=q_codes[:].bitcast(FP8X4), rhs_scale=q_scales[:], start=True, stop=True)
+            nc.scalar.activation(out=dist[b][:], in_=a[:], func=ACT.Identity, bias=kn_col[:, b:b + 1], scale=-2.0)
+
+        def turn(i):
+            for j in range(2):
+                nc.tensor.transpose(turned[i][:, j, :], dist[2 * i + j][:], ident[:])
+            nc.vector.tensor_reduce(out=nearest[:, 16 * i:16 * (i + 1)],
+                                    in_=turned[i][:, 0:2, :].rearrange("p j (c s) -> p (j c) s", s=SEG),
+                                    axis=AX.X, op=ALU.min)
+
+        for b in range(4):
+            score(b)
+        turn(0)
+        turn(1)
+        for b in range(4, 8):
+            score(b)
+        turn(2)
+        turn(3)
+
+        result = keep.tile([P, N // SEG], F32, name="result")
+        nc.vector.tensor_scalar(out=result[:], in0=nearest[:], scalar1=qn_col[:], scalar2=None, op0=ALU.add)
+        nc.sync.dma_start(out=out[0], in_=result[:])

@@ -28,12 +28,15 @@ FLOPS = 2 * NQ * N * D
 BYTES = T * D + 16 * T + 4 * T + 4 * D * NQ + 4 * NQ + 2 * N * 8 + 4 * NQ * (N // SEG)
 
 
+WORDS_FIRST = 1536
+PIECE = 256
+
+
 def tile_attend_celldist_kernel(tc, qT, k_words, k_scales, kn, qn, offs, out):
     nc = tc.nc
     with ExitStack() as ctx:
         keep = ctx.enter_context(tc.tile_pool(name="keep", bufs=1))
-        psum_a = ctx.enter_context(tc.psum_pool(name="psum_a", bufs=4))
-        psum_t = ctx.enter_context(tc.psum_pool(name="psum_t", bufs=1))
+        psum = ctx.enter_context(tc.psum_pool(name="psum", bufs=1))
 
         offsets = keep.tile([P, N // 16], U16, name="offsets")
         scale_table = keep.tile([P, T], U8, name="scale_table", align_bytes=64)
@@ -42,20 +45,22 @@ def tile_attend_celldist_kernel(tc, qT, k_words, k_scales, kn, qn, offs, out):
         q_raw = keep.tile([P, 4, NQ], F32, name="q_raw")
         qn_col = keep.tile([P, 1], F32, name="qn_col")
         ident = keep.tile([P, P], F32, name="ident")
+        words = k_words[0].rearrange("p n t -> p (n t)").bitcast(I32)
 
         nc.vector.memset(scale_table[:].bitcast(I32), 0)
-        nc.sync.dma_start(offsets[:], offs)
         nc.sync.dma_start(out=q_raw[:], in_=qT[0].rearrange("(p j) q -> p j q", j=4))
-        nc.sync.dma_start(out=word_table[:], in_=k_words[0].rearrange("p n t -> p (n t)").bitcast(I32))
+        nc.sync.dma_start(out=kn_table[KN_ROW:P, :], in_=kn[0:1, :])
+        nc.sync.dma_start(offsets[:], offs)
         nc.sync.dma_start(out=qn_col[:], in_=qn[0])
-        nc.scalar.dma_start(out=kn_table[KN_ROW:P, :], in_=kn[0:1, :])
+        nc.sync.dma_start(out=word_table[:, 0:WORDS_FIRST], in_=words[:, 0:WORDS_FIRST])
         for r in range(4):
-            nc.scalar.dma_start(out=scale_table[r:P:32, :].bitcast(I32), in_=k_scales[0][r:16:4, :].bitcast(I32))
-        nc.vector.memset(kn_table[0:KN_ROW, :], 0.0)
+            nc.sync.dma_start(out=scale_table[r:P:32, :].bitcast(I32), in_=k_scales[0][r:16:4, :].bitcast(I32))
+        nc.sync.dma_start(out=word_table[:, WORDS_FIRST:T], in_=words[:, WORDS_FIRST:T])
+        nc.vector.memset(kn_table[0:KN_ROW, :].bitcast(I32), 0)
         make_identity(nc, ident[:])
 
         q_bf = keep.tile([P, NQ, 4], BF16, name="q_bf", align_bytes=64)
-        nc.scalar.copy(out=q_bf[:], in_=q_raw[:].rearrange("p j q -> p q j"))
+        nc.scalar.activation(out=q_bf[:], in_=q_raw[:].rearrange("p j q -> p q j"), func=ACT.Identity)
 
         kn_g = keep.tile([P, N], F32, name="kn_g")
         nc.vector.tensor_copy(kn_g[:], kn_table[:].indirect(offsets[:]))
@@ -67,45 +72,46 @@ def tile_attend_celldist_kernel(tc, qT, k_words, k_scales, kn, qn, offs, out):
         scale_g = keep.tile([P, N], U8, name="scale_g", align_bytes=64)
         nc.vector.tensor_copy(scale_g[:], scale_table[:].indirect(offsets[:]))
 
-        turned = [psum_t.tile([P, 4, P], F32, name=f"turned{i}") for i in range(4)]
         kn_col = keep.tile([P, BLOCKS], F32, name="kn_col")
         for h in range(2):
+            turned = psum.tile([P, 4, P], F32, name=f"turned{h}")
             for j in range(4):
                 b = 4 * h + j
-                nc.tensor.transpose(turned[h][:, j, :], kn_g[:, b * P:(b + 1) * P], ident[:])
-            nc.scalar.copy(out=kn_col[:, 4 * h:4 * h + 4], in_=turned[h][:, :, KN_ROW])
+                nc.tensor.transpose(turned[:, j, :], kn_g[:, b * P:(b + 1) * P], ident[:])
+            nc.scalar.copy(out=kn_col[:, 4 * h:4 * h + 4], in_=turned[:, :, KN_ROW])
+        norms = [keep.tile([P, HALF], F32, name=f"norms{h}") for h in range(2)]
+        for h in range(2):
+            spread = psum.tile([P, 4, P], F32, name=f"spread{h}")
+            for j in range(4):
+                b = 4 * h + j
+                nc.tensor.transpose(spread[:, j, :], kn_col[:, b:b + 1].to_broadcast([P, P]), ident[:])
+            nc.scalar.activation(out=norms[h][:], in_=spread[:].rearrange("p j s -> p (j s)"), func=ACT.Identity, bias=qn_col[:])
 
         word_g = [keep.tile([P, HALF], U32, name=f"word_g{h}", align_bytes=64) for h in range(2)]
         for h in range(2):
             nc.vector.tensor_copy(word_g[h][:], word_table[:].bitcast(U32).indirect(offsets[:, 32 * h:32 * (h + 1)]))
 
-        dist = [keep.tile([P, NQ], F32, name=f"dist{b}") for b in range(BLOCKS)]
-        nearest = keep.tile([P, N // SEG], F32, name="nearest")
+        dots = [psum.tile([P, PIECE], F32, name=f"dots{i}") for i in range(4)]
+        dist = [keep.tile([P, PIECE], F32, name=f"dist{i}") for i in range(4)]
+        result = keep.tile([P, N // SEG], F32, name="result")
+        for i in range(4):
+            h, j = divmod(i, 2)
+            nc.tensor.matmul_mx(out=dots[i][:], lhsT=q_codes[:].bitcast(FP8X4), lhsT_scale=q_scales[:],
+                                rhs=word_g[h][:, j * PIECE:(j + 1) * PIECE].bitcast(FP8X4),
+                                rhs_scale=scale_g[:, i * PIECE:(i + 1) * PIECE], start=True, stop=True)
 
-        def score(b):
-            h, j = divmod(b, 4)
-            a = psum_a.tile([P, NQ], F32, name="a")
-            nc.tensor.matmul_mx(out=a[:], lhsT=word_g[h][:, j * P:(j + 1) * P].bitcast(FP8X4),
-                                lhsT_scale=scale_g[:, b * P:(b + 1) * P],
-                                rhs=q_codes[:].bitcast(FP8X4), rhs_scale=q_scales[:], start=True, stop=True)
-            nc.scalar.activation(out=dist[b][:], in_=a[:], func=ACT.Identity, bias=kn_col[:, b:b + 1], scale=-2.0)
+        def distance(i):
+            h, j = divmod(i, 2)
+            nc.vector.scalar_tensor_tensor(out=dist[i][:], in0=dots[i][:], scalar=-2.0,
+                                           in1=norms[h][:, j * PIECE:(j + 1) * PIECE], op0=ALU.mult, op1=ALU.add)
 
-        def turn(i):
-            for j in range(2):
-                nc.tensor.transpose(turned[i][:, j, :], dist[2 * i + j][:], ident[:])
-            nc.vector.tensor_reduce(out=nearest[:, 16 * i:16 * (i + 1)],
-                                    in_=turned[i][:, 0:2, :].rearrange("p j (c s) -> p (j c) s", s=SEG),
+        def nearest(i):
+            nc.vector.tensor_reduce(out=result[:, 16 * i:16 * (i + 1)], in_=dist[i][:].rearrange("p (c s) -> p c s", s=SEG),
                                     axis=AX.X, op=ALU.min)
 
-        for b in range(4):
-            score(b)
-        turn(0)
-        turn(1)
-        for b in range(4, 8):
-            score(b)
-        turn(2)
-        turn(3)
-
-        result = keep.tile([P, N // SEG], F32, name="result")
-        nc.vector.tensor_scalar(out=result[:], in0=nearest[:], scalar1=qn_col[:], scalar2=None, op0=ALU.add)
+        distance(0)
+        for i in range(1, 4):
+            distance(i)
+            nearest(i - 1)
+        nearest(3)
         nc.sync.dma_start(out=out[0], in_=result[:])

@@ -28,7 +28,8 @@ FLOPS = 2 * NQ * N * D
 BYTES = T * D + 16 * T + 4 * T + 4 * D * NQ + 4 * NQ + 2 * N * 8 + 4 * NQ * (N // SEG)
 
 
-WORDS_FIRST = 1536
+WORDS_FIRST = 768
+KN_V = 2096
 PIECE = 256
 
 
@@ -47,16 +48,22 @@ def tile_attend_celldist_kernel(tc, qT, k_words, k_scales, kn, qn, offs, out):
         ident = keep.tile([P, P], F32, name="ident")
         words = k_words[0].rearrange("p n t -> p (n t)").bitcast(I32)
 
-        nc.vector.memset(scale_table[:].bitcast(I32), 0)
-        nc.sync.dma_start(out=q_raw[:], in_=qT[0].rearrange("(p j) q -> p j q", j=4))
+        scale_words = scale_table[:].bitcast(I32)
+        kn_rest = kn_table[0:KN_ROW, :]
+        nc.vector.memset(scale_words[:, 0:257], 0)
+        nc.vector.memset(scale_words[:, 257:512], 0)
+        nc.gpsimd.memset(scale_words[:, 512:1024], 0)
         nc.sync.dma_start(out=kn_table[KN_ROW:P, :], in_=kn[0:1, :])
         nc.sync.dma_start(offsets[:], offs)
-        nc.sync.dma_start(out=qn_col[:], in_=qn[0])
+        nc.sync.dma_start(out=q_raw[:], in_=qT[0].rearrange("(p j) q -> p j q", j=4))
         nc.sync.dma_start(out=word_table[:, 0:WORDS_FIRST], in_=words[:, 0:WORDS_FIRST])
         for r in range(4):
             nc.sync.dma_start(out=scale_table[r:P:32, :].bitcast(I32), in_=k_scales[0][r:16:4, :].bitcast(I32))
         nc.sync.dma_start(out=word_table[:, WORDS_FIRST:T], in_=words[:, WORDS_FIRST:T])
-        nc.vector.memset(kn_table[0:KN_ROW, :].bitcast(I32), 0)
+        nc.sync.dma_start(out=qn_col[:], in_=qn[0])
+        nc.vector.memset(kn_rest[:, 0:KN_V // 2 - 1].bitcast(I32), 0)
+        nc.vector.memset(kn_rest[:, KN_V // 2 - 1:KN_V].bitcast(I32), 0)
+        nc.gpsimd.memset(kn_rest[:, KN_V:T].bitcast(I32), 0)
         make_identity(nc, ident[:])
 
         q_bf = keep.tile([P, NQ, 4], BF16, name="q_bf", align_bytes=64)
@@ -65,12 +72,12 @@ def tile_attend_celldist_kernel(tc, qT, k_words, k_scales, kn, qn, offs, out):
         kn_g = keep.tile([P, N], F32, name="kn_g")
         nc.vector.tensor_copy(kn_g[:], kn_table[:].indirect(offsets[:]))
 
+        scale_g = keep.tile([P, N], U8, name="scale_g", align_bytes=64)
+        nc.vector.tensor_copy(scale_g[:], scale_table[:].indirect(offsets[:]))
+
         q_codes = keep.tile([P, NQ], U32, name="q_codes", align_bytes=64)
         q_scales = keep.tile([P, NQ], U8, name="q_scales", align_bytes=64)
         nc.vector.quantize_mx(out=q_codes[:].bitcast(FP8X4), scales=q_scales[:], in_=q_bf[:].rearrange("p q j -> p (q j)"))
-
-        scale_g = keep.tile([P, N], U8, name="scale_g", align_bytes=64)
-        nc.vector.tensor_copy(scale_g[:], scale_table[:].indirect(offsets[:]))
 
         kn_col = keep.tile([P, BLOCKS], F32, name="kn_col")
         for h in range(2):

@@ -28,7 +28,6 @@ FLOPS = 2 * NQ * N * D
 BYTES = T * D + 16 * T + 4 * T + 4 * D * NQ + 4 * NQ + 2 * N * 8 + 4 * NQ * (N // SEG)
 
 
-WORDS_FIRST = 768
 KN_V = 2096
 PIECE = 256
 
@@ -45,6 +44,7 @@ def tile_attend_celldist_kernel(tc, qT, k_words, k_scales, kn, qn, offs, out):
         word_table = keep.tile([P, T], I32, name="word_table")
         q_raw = keep.tile([P, 4, NQ], F32, name="q_raw")
         qn_col = keep.tile([P, 1], F32, name="qn_col")
+        scale_plane = keep.tile([P, N], U8, name="scale_plane", align_bytes=64)
         ident = keep.tile([P, P], F32, name="ident")
         words = k_words[0].rearrange("p n t -> p (n t)").bitcast(I32)
 
@@ -53,18 +53,17 @@ def tile_attend_celldist_kernel(tc, qT, k_words, k_scales, kn, qn, offs, out):
         nc.vector.memset(scale_words[:, 0:257], 0)
         nc.vector.memset(scale_words[:, 257:512], 0)
         nc.gpsimd.memset(scale_words[:, 512:1024], 0)
+        nc.sync.dma_start(out=q_raw[:], in_=qT[0].rearrange("(p j) q -> p j q", j=4))
         nc.sync.dma_start(out=kn_table[KN_ROW:P, :], in_=kn[0:1, :])
         nc.sync.dma_start(offsets[:], offs)
-        nc.sync.dma_start(out=q_raw[:], in_=qT[0].rearrange("(p j) q -> p j q", j=4))
-        nc.sync.dma_start(out=word_table[:, 0:WORDS_FIRST], in_=words[:, 0:WORDS_FIRST])
-        for r in range(4):
-            nc.sync.dma_start(out=scale_table[r:P:32, :].bitcast(I32), in_=k_scales[0][r:16:4, :].bitcast(I32))
-        nc.sync.dma_start(out=word_table[:, WORDS_FIRST:T], in_=words[:, WORDS_FIRST:T])
         nc.sync.dma_start(out=qn_col[:], in_=qn[0])
+        nc.sync.dma_start(out=scale_table[4:P:8, :].bitcast(I32), in_=k_scales[0].bitcast(I32))
+        nc.sync.dma_start(out=word_table[:], in_=words)
         nc.vector.memset(kn_rest[:, 0:KN_V // 2 - 1].bitcast(I32), 0)
         nc.vector.memset(kn_rest[:, KN_V // 2 - 1:KN_V].bitcast(I32), 0)
         nc.gpsimd.memset(kn_rest[:, KN_V:T].bitcast(I32), 0)
         make_identity(nc, ident[:])
+        nc.gpsimd.memset(scale_plane[:].bitcast(I32), 0)
 
         q_bf = keep.tile([P, NQ, 4], BF16, name="q_bf", align_bytes=64)
         nc.scalar.activation(out=q_bf[:], in_=q_raw[:].rearrange("p j q -> p q j"), func=ACT.Identity)
@@ -74,6 +73,8 @@ def tile_attend_celldist_kernel(tc, qT, k_words, k_scales, kn, qn, offs, out):
 
         scale_g = keep.tile([P, N], U8, name="scale_g", align_bytes=64)
         nc.vector.tensor_copy(scale_g[:], scale_table[:].indirect(offsets[:]))
+        for r in range(4):
+            nc.sync.dma_start(out=scale_plane[r:P:32, :].bitcast(I32), in_=scale_g[4 + 8 * r:P:32, :].bitcast(I32))
 
         q_codes = keep.tile([P, NQ], U32, name="q_codes", align_bytes=64)
         q_scales = keep.tile([P, NQ], U8, name="q_scales", align_bytes=64)
@@ -105,7 +106,7 @@ def tile_attend_celldist_kernel(tc, qT, k_words, k_scales, kn, qn, offs, out):
             h, j = divmod(i, 2)
             nc.tensor.matmul_mx(out=dots[i][:], lhsT=q_codes[:].bitcast(FP8X4), lhsT_scale=q_scales[:],
                                 rhs=word_g[h][:, j * PIECE:(j + 1) * PIECE].bitcast(FP8X4),
-                                rhs_scale=scale_g[:, i * PIECE:(i + 1) * PIECE], start=True, stop=True)
+                                rhs_scale=scale_plane[:, i * PIECE:(i + 1) * PIECE], start=True, stop=True)
 
         def distance(i):
             h, j = divmod(i, 2)

@@ -21,14 +21,14 @@ NQ = 128
 D = 512
 SEG = 16
 HALF = 512
-BLOCKS = N // P
 KN_ROW = P - 1
+PLANE_ROW = 4
 
 FLOPS = 2 * NQ * N * D
 BYTES = T * D + 16 * T + 4 * T + 4 * D * NQ + 4 * NQ + 2 * N * 8 + 4 * NQ * (N // SEG)
 
 
-KN_V = 2096
+KN_V = 1856
 PIECE = 256
 
 
@@ -36,90 +36,90 @@ def tile_attend_celldist_kernel(tc, qT, k_words, k_scales, kn, qn, offs, out):
     nc = tc.nc
     with ExitStack() as ctx:
         keep = ctx.enter_context(tc.tile_pool(name="keep", bufs=1))
+        shared = ctx.enter_context(tc.tile_pool(name="shared", bufs=1))
         psum = ctx.enter_context(tc.psum_pool(name="psum", bufs=1))
 
         offsets = keep.tile([P, N // 16], U16, name="offsets")
-        scale_table = keep.tile([P, T], U8, name="scale_table", align_bytes=64)
+        scale_table = shared.tile([P, T], U8, name="scale_table", align_bytes=64, offset=0)
         kn_table = keep.tile([P, T], F32, name="kn_table")
         word_table = keep.tile([P, T], I32, name="word_table")
         q_raw = keep.tile([P, 4, NQ], F32, name="q_raw")
         qn_col = keep.tile([P, 1], F32, name="qn_col")
-        scale_plane = keep.tile([P, N], U8, name="scale_plane", align_bytes=64)
+        scale_plane = [keep.tile([P, HALF], U8, name=f"scale_plane{h}", align_bytes=64) for h in range(2)]
         ident = keep.tile([P, P], F32, name="ident")
         words = k_words[0].rearrange("p n t -> p (n t)").bitcast(I32)
 
         scale_words = scale_table[:].bitcast(I32)
-        kn_rest = kn_table[0:KN_ROW, :]
+        kn_rest = kn_table[0:KN_ROW, :].bitcast(I32)
         nc.vector.memset(scale_words[:, 0:257], 0)
         nc.vector.memset(scale_words[:, 257:512], 0)
         nc.gpsimd.memset(scale_words[:, 512:1024], 0)
-        nc.sync.dma_start(out=q_raw[:], in_=qT[0].rearrange("(p j) q -> p j q", j=4))
         nc.sync.dma_start(out=kn_table[KN_ROW:P, :], in_=kn[0:1, :])
         nc.sync.dma_start(offsets[:], offs)
-        nc.sync.dma_start(out=qn_col[:], in_=qn[0])
-        nc.sync.dma_start(out=scale_table[4:P:8, :].bitcast(I32), in_=k_scales[0].bitcast(I32))
+        nc.sync.dma_start(out=q_raw[:], in_=qT[0].rearrange("(p j) q -> p j q", j=4))
+        nc.sync.dma_start(out=scale_table[11:11 + 7 * 15 + 1:7, :].bitcast(I32), in_=k_scales[0].bitcast(I32))
         nc.sync.dma_start(out=word_table[:], in_=words)
-        nc.vector.memset(kn_rest[:, 0:KN_V // 2 - 1].bitcast(I32), 0)
-        nc.vector.memset(kn_rest[:, KN_V // 2 - 1:KN_V].bitcast(I32), 0)
-        nc.gpsimd.memset(kn_rest[:, KN_V:T].bitcast(I32), 0)
+        nc.sync.dma_start(out=qn_col[:], in_=qn[0])
+        nc.vector.memset(kn_rest[:, 0:KN_V // 2 - 1], 0)
+        nc.vector.memset(kn_rest[:, KN_V // 2 - 1:KN_V], 0)
+        nc.gpsimd.memset(kn_rest[:, KN_V:T], 0)
         make_identity(nc, ident[:])
-        nc.gpsimd.memset(scale_plane[:].bitcast(I32), 0)
+        for h in range(2):
+            nc.gpsimd.memset(scale_plane[h][:].bitcast(I32), 0)
 
         q_bf = keep.tile([P, NQ, 4], BF16, name="q_bf", align_bytes=64)
         nc.scalar.activation(out=q_bf[:], in_=q_raw[:].rearrange("p j q -> p q j"), func=ACT.Identity)
 
-        kn_g = keep.tile([P, N], F32, name="kn_g")
-        nc.vector.tensor_copy(kn_g[:], kn_table[:].indirect(offsets[:]))
+        norms = [keep.tile([P, PIECE], F32, name=f"norms{i}") for i in range(4)]
 
-        scale_g = keep.tile([P, N], U8, name="scale_g", align_bytes=64)
-        nc.vector.tensor_copy(scale_g[:], scale_table[:].indirect(offsets[:]))
-        for r in range(4):
-            nc.sync.dma_start(out=scale_plane[r:P:32, :].bitcast(I32), in_=scale_g[4 + 8 * r:P:32, :].bitcast(I32))
+        def spread_norms(h, kn_g):
+            turned = psum.tile([P, 4, P], F32, name=f"turned{h}", tag=f"kn_bank{2 * h}")
+            for j in range(4):
+                nc.tensor.transpose(turned[:, j, :], kn_g[:, j * P:(j + 1) * P], ident[:])
+            kn_col = keep.tile([P, 4], F32, name=f"kn_col{h}")
+            nc.scalar.copy(out=kn_col[:], in_=turned[:, :, KN_ROW])
+            for i in range(2):
+                spread = psum.tile([P, 2, P], F32, name=f"spread{h}{i}", tag=f"kn_bank{2 * h + 1 - i}")
+                for j in range(2):
+                    nc.tensor.transpose(spread[:, j, :], kn_col[:, 2 * i + j:2 * i + j + 1].to_broadcast([P, P]), ident[:])
+                nc.scalar.activation(out=norms[2 * h + i][:], in_=spread[:].rearrange("p j s -> p (j s)"),
+                                     func=ACT.Identity, bias=qn_col[:])
+
+        kn_g0 = keep.tile([P, HALF], F32, name="kn_g0")
+        nc.vector.tensor_copy(kn_g0[:], kn_table[:].indirect(offsets[:, 0:32]))
+        kn_g1 = keep.tile([P, HALF], F32, name="kn_g1")
+        nc.vector.tensor_copy(kn_g1[:], kn_table[:].indirect(offsets[:, 32:64]))
+        spread_norms(0, kn_g0)
+        spread_norms(1, kn_g1)
+
+        scale_g = [keep.tile([P, HALF], U8, name=f"scale_g{h}", align_bytes=64) for h in range(2)]
+        for h in range(2):
+            nc.vector.tensor_copy(scale_g[h][:], scale_table[:].indirect(offsets[:, 32 * h:32 * (h + 1)]))
+            for r in range(4):
+                nc.sync.dma_start(out=scale_plane[h][PLANE_ROW + r:P:32, :].bitcast(I32), in_=scale_g[h][11 + 7 * r:11 + 7 * r + 28 * 3 + 1:28, :].bitcast(I32))
 
         q_codes = keep.tile([P, NQ], U32, name="q_codes", align_bytes=64)
         q_scales = keep.tile([P, NQ], U8, name="q_scales", align_bytes=64)
         nc.vector.quantize_mx(out=q_codes[:].bitcast(FP8X4), scales=q_scales[:], in_=q_bf[:].rearrange("p q j -> p (q j)"))
 
-        kn_col = keep.tile([P, BLOCKS], F32, name="kn_col")
-        for h in range(2):
-            turned = psum.tile([P, 4, P], F32, name=f"turned{h}")
-            for j in range(4):
-                b = 4 * h + j
-                nc.tensor.transpose(turned[:, j, :], kn_g[:, b * P:(b + 1) * P], ident[:])
-            nc.scalar.copy(out=kn_col[:, 4 * h:4 * h + 4], in_=turned[:, :, KN_ROW])
-        norms = [keep.tile([P, HALF], F32, name=f"norms{h}") for h in range(2)]
-        for h in range(2):
-            spread = psum.tile([P, 4, P], F32, name=f"spread{h}")
-            for j in range(4):
-                b = 4 * h + j
-                nc.tensor.transpose(spread[:, j, :], kn_col[:, b:b + 1].to_broadcast([P, P]), ident[:])
-            nc.scalar.activation(out=norms[h][:], in_=spread[:].rearrange("p j s -> p (j s)"), func=ACT.Identity, bias=qn_col[:])
-
-        word_g = [keep.tile([P, HALF], U32, name=f"word_g{h}", align_bytes=64) for h in range(2)]
+        word_g = [shared.tile([P, HALF], U32, name=f"word_g{h}", align_bytes=64, offset=4 * HALF * h) for h in range(2)]
         for h in range(2):
             nc.vector.tensor_copy(word_g[h][:], word_table[:].bitcast(U32).indirect(offsets[:, 32 * h:32 * (h + 1)]))
 
         dots = [psum.tile([P, PIECE], F32, name=f"dots{i}") for i in range(4)]
-        dist = [keep.tile([P, PIECE], F32, name=f"dist{i}") for i in range(4)]
         result = keep.tile([P, N // SEG], F32, name="result")
         for i in range(4):
             h, j = divmod(i, 2)
             nc.tensor.matmul_mx(out=dots[i][:], lhsT=q_codes[:].bitcast(FP8X4), lhsT_scale=q_scales[:],
                                 rhs=word_g[h][:, j * PIECE:(j + 1) * PIECE].bitcast(FP8X4),
-                                rhs_scale=scale_plane[:, i * PIECE:(i + 1) * PIECE], start=True, stop=True)
+                                rhs_scale=scale_plane[h][PLANE_ROW:P, j * PIECE:(j + 1) * PIECE], start=True, stop=True)
 
-        def distance(i):
-            h, j = divmod(i, 2)
-            nc.vector.scalar_tensor_tensor(out=dist[i][:], in0=dots[i][:], scalar=-2.0,
-                                           in1=norms[h][:, j * PIECE:(j + 1) * PIECE], op0=ALU.mult, op1=ALU.add)
-
-        def nearest(i):
-            nc.vector.tensor_reduce(out=result[:, 16 * i:16 * (i + 1)], in_=dist[i][:].rearrange("p (c s) -> p c s", s=SEG),
-                                    axis=AX.X, op=ALU.min)
-
-        distance(0)
-        for i in range(1, 4):
-            distance(i)
-            nearest(i - 1)
-        nearest(3)
+        for h in range(2):
+            dist = {i: keep.tile([P, PIECE], F32, name=f"dist{i}", tag=f"dist{i % 2}") for i in (2 * h, 2 * h + 1)}
+            for i in (2 * h, 2 * h + 1):
+                nc.vector.scalar_tensor_tensor(out=dist[i][:], in0=dots[i][:], scalar=-2.0, in1=norms[i][:],
+                                               op0=ALU.mult, op1=ALU.add)
+            for i in (2 * h, 2 * h + 1):
+                nc.vector.tensor_reduce(out=result[:, 16 * i:16 * (i + 1)], in_=dist[i][:].rearrange("p (c s) -> p c s", s=SEG),
+                                        axis=AX.X, op=ALU.min)
         nc.sync.dma_start(out=out[0], in_=result[:])

@@ -57,8 +57,9 @@ def tile_attend_celldist_kernel(tc, qT, k_words, k_scales, kn, qn, offs, out):
         nc.sync.dma_start(out=kn_table[KN_ROW:P, :], in_=kn[0:1, :])
         nc.sync.dma_start(offsets[:], offs)
         nc.sync.dma_start(out=q_raw[:], in_=qT[0].rearrange("(p j) q -> p j q", j=4))
-        nc.sync.dma_start(out=scale_table[11:11 + 7 * 15 + 1:7, :].bitcast(I32), in_=k_scales[0].bitcast(I32))
-        nc.sync.dma_start(out=word_table[:], in_=words)
+        nc.sync.dma_start(out=word_table[:, 0:512], in_=words[:, 0:512])
+        nc.sync.dma_start(out=scale_table[0:0 + 7 * 15 + 1:7, :].bitcast(I32), in_=k_scales[0].bitcast(I32))
+        nc.sync.dma_start(out=word_table[:, 512:T], in_=words[:, 512:T])
         nc.sync.dma_start(out=qn_col[:], in_=qn[0])
         nc.vector.memset(kn_rest[:, 0:KN_V // 2 - 1], 0)
         nc.vector.memset(kn_rest[:, KN_V // 2 - 1:KN_V], 0)
@@ -96,7 +97,7 @@ def tile_attend_celldist_kernel(tc, qT, k_words, k_scales, kn, qn, offs, out):
         for h in range(2):
             nc.vector.tensor_copy(scale_g[h][:], scale_table[:].indirect(offsets[:, 32 * h:32 * (h + 1)]))
             for r in range(4):
-                nc.sync.dma_start(out=scale_plane[h][PLANE_ROW + r:P:32, :].bitcast(I32), in_=scale_g[h][11 + 7 * r:11 + 7 * r + 28 * 3 + 1:28, :].bitcast(I32))
+                nc.sync.dma_start(out=scale_plane[h][PLANE_ROW + r:P:32, :].bitcast(I32), in_=scale_g[h][0 + 7 * r:0 + 7 * r + 28 * 3 + 1:28, :].bitcast(I32))
 
         q_codes = keep.tile([P, NQ], U32, name="q_codes", align_bytes=64)
         q_scales = keep.tile([P, NQ], U8, name="q_scales", align_bytes=64)

@@ -28,7 +28,7 @@ FLOPS = 2 * NQ * N * D
 BYTES = T * D + 16 * T + 4 * T + 4 * D * NQ + 4 * NQ + 2 * N * 8 + 4 * NQ * (N // SEG)
 
 
-KN_V = 1856
+KN_V = 1984
 PIECE = 256
 
 
@@ -86,12 +86,10 @@ def tile_attend_celldist_kernel(tc, qT, k_words, k_scales, kn, qn, offs, out):
                 nc.scalar.activation(out=norms[2 * h + i][:], in_=spread[:].rearrange("p j s -> p (j s)"),
                                      func=ACT.Identity, bias=qn_col[:])
 
-        kn_g0 = keep.tile([P, HALF], F32, name="kn_g0")
-        nc.vector.tensor_copy(kn_g0[:], kn_table[:].indirect(offsets[:, 0:32]))
-        kn_g1 = keep.tile([P, HALF], F32, name="kn_g1")
-        nc.vector.tensor_copy(kn_g1[:], kn_table[:].indirect(offsets[:, 32:64]))
-        spread_norms(0, kn_g0)
-        spread_norms(1, kn_g1)
+        kn_g = keep.tile([P, N], F32, name="kn_g")
+        nc.vector.tensor_copy(kn_g[:], kn_table[:].indirect(offsets[:]))
+        for h in range(2):
+            spread_norms(h, kn_g[:, h * HALF:(h + 1) * HALF])
 
         scale_g = [keep.tile([P, HALF], U8, name=f"scale_g{h}", align_bytes=64) for h in range(2)]
         for h in range(2):
@@ -103,7 +101,7 @@ def tile_attend_celldist_kernel(tc, qT, k_words, k_scales, kn, qn, offs, out):
         q_scales = keep.tile([P, NQ], U8, name="q_scales", align_bytes=64)
         nc.vector.quantize_mx(out=q_codes[:].bitcast(FP8X4), scales=q_scales[:], in_=q_bf[:].rearrange("p q j -> p (q j)"))
 
-        word_g = [shared.tile([P, HALF], U32, name=f"word_g{h}", align_bytes=64, offset=4 * HALF * h) for h in range(2)]
+        word_g = [keep.tile([P, HALF], U32, name=f"word_g{h}", align_bytes=64) for h in range(2)]
         for h in range(2):
             nc.vector.tensor_copy(word_g[h][:], word_table[:].bitcast(U32).indirect(offsets[:, 32 * h:32 * (h + 1)]))
 

@@ -28,7 +28,6 @@ FLOPS = 2 * NQ * N * D
 BYTES = T * D + 16 * T + 4 * T + 4 * D * NQ + 4 * NQ + 2 * N * 8 + 4 * NQ * (N // SEG)
 
 
-KN_V = 1984
 PIECE = 256
 
 
@@ -51,9 +50,7 @@ def tile_attend_celldist_kernel(tc, qT, k_words, k_scales, kn, qn, offs, out):
 
         scale_words = scale_table[:].bitcast(I32)
         kn_rest = kn_table[0:KN_ROW, :].bitcast(I32)
-        nc.vector.memset(scale_words[:, 0:257], 0)
-        nc.vector.memset(scale_words[:, 257:512], 0)
-        nc.gpsimd.memset(scale_words[:, 512:1024], 0)
+        nc.vector.memset(scale_words, 0)
         nc.sync.dma_start(out=kn_table[KN_ROW:P, :], in_=kn[0:1, :])
         nc.sync.dma_start(offsets[:], offs)
         nc.sync.dma_start(out=q_raw[:], in_=qT[0].rearrange("(p j) q -> p j q", j=4))
@@ -61,12 +58,11 @@ def tile_attend_celldist_kernel(tc, qT, k_words, k_scales, kn, qn, offs, out):
         nc.sync.dma_start(out=scale_table[0:0 + 7 * 15 + 1:7, :].bitcast(I32), in_=k_scales[0].bitcast(I32))
         nc.sync.dma_start(out=word_table[:, 512:T], in_=words[:, 512:T])
         nc.sync.dma_start(out=qn_col[:], in_=qn[0])
-        nc.vector.memset(kn_rest[:, 0:KN_V // 2 - 1], 0)
-        nc.vector.memset(kn_rest[:, KN_V // 2 - 1:KN_V], 0)
-        nc.gpsimd.memset(kn_rest[:, KN_V:T], 0)
-        make_identity(nc, ident[:])
+        nc.vector.memset(kn_rest, 0)
         for h in range(2):
-            nc.gpsimd.memset(scale_plane[h][:].bitcast(I32), 0)
+            nc.vector.memset(scale_plane[h][:].bitcast(I32), 0)
+        nc.vector.memset(ident[:], 0.0)
+        make_identity(nc, ident[:], nomemset=True)
 
         q_bf = keep.tile([P, NQ, 4], BF16, name="q_bf", align_bytes=64)
         nc.scalar.activation(out=q_bf[:], in_=q_raw[:].rearrange("p j q -> p q j"), func=ACT.Identity)

@@ -53,10 +53,9 @@ def tile_attend_celldist_kernel(tc, qT, k_words, k_scales, kn, qn, offs, out):
         nc.vector.memset(scale_words, 0)
         nc.sync.dma_start(out=kn_table[KN_ROW:P, :], in_=kn[0:1, :])
         nc.sync.dma_start(offsets[:], offs)
-        nc.sync.dma_start(out=q_raw[:], in_=qT[0].rearrange("(p j) q -> p j q", j=4))
-        nc.sync.dma_start(out=word_table[:, 0:512], in_=words[:, 0:512])
+        nc.scalar.dma_start(out=q_raw[:], in_=qT[0].rearrange("(p j) q -> p j q", j=4))
         nc.sync.dma_start(out=scale_table[0:0 + 7 * 15 + 1:7, :].bitcast(I32), in_=k_scales[0].bitcast(I32))
-        nc.sync.dma_start(out=word_table[:, 512:T], in_=words[:, 512:T])
+        nc.sync.dma_start(out=word_table[:], in_=words)
         nc.sync.dma_start(out=qn_col[:], in_=qn[0])
         nc.vector.memset(kn_rest, 0)
         for h in range(2):
@@ -70,30 +69,32 @@ def tile_attend_celldist_kernel(tc, qT, k_words, k_scales, kn, qn, offs, out):
         norms = [keep.tile([P, PIECE], F32, name=f"norms{i}") for i in range(4)]
 
         def spread_norms(h, kn_g):
-            turned = psum.tile([P, 4, P], F32, name=f"turned{h}", tag=f"kn_bank{2 * h}")
-            for j in range(4):
-                nc.tensor.transpose(turned[:, j, :], kn_g[:, j * P:(j + 1) * P], ident[:])
+            nc.vector.tensor_copy(kn_g[:], kn_table[:].indirect(offsets[:, 32 * h:32 * (h + 1)]))
             kn_col = keep.tile([P, 4], F32, name=f"kn_col{h}")
-            nc.scalar.copy(out=kn_col[:], in_=turned[:, :, KN_ROW])
+            for j in range(4):
+                turned = psum.tile([P, P], F32, name=f"turned{h}{j}", tag=f"dots{j}")
+                nc.tensor.transpose(turned[:], kn_g[:, j * P:(j + 1) * P], ident[:])
+                nc.scalar.copy(out=kn_col[:, j:j + 1], in_=turned[:, KN_ROW:P])
             for i in range(2):
-                spread = psum.tile([P, 2, P], F32, name=f"spread{h}{i}", tag=f"kn_bank{2 * h + 1 - i}")
+                spread = psum.tile([P, 2, P], F32, name=f"spread{h}{i}")
                 for j in range(2):
                     nc.tensor.transpose(spread[:, j, :], kn_col[:, 2 * i + j:2 * i + j + 1].to_broadcast([P, P]), ident[:])
-                nc.scalar.activation(out=norms[2 * h + i][:], in_=spread[:].rearrange("p j s -> p (j s)"),
-                                     func=ACT.Identity, bias=qn_col[:])
+                flat = spread[:].rearrange("p j s -> p (j s)")
+                if h == 0:
+                    nc.scalar.copy(out=norms[i][:], in_=flat)
+                else:
+                    nc.scalar.activation(out=norms[2 + i][:], in_=flat, func=ACT.Identity, bias=qn_col[:])
 
-        kn_g = keep.tile([P, N], F32, name="kn_g")
-        nc.vector.tensor_copy(kn_g[:], kn_table[:].indirect(offsets[:]))
         for h in range(2):
-            spread_norms(h, kn_g[:, h * HALF:(h + 1) * HALF])
-
-        scale_g = [keep.tile([P, HALF], U8, name=f"scale_g{h}", align_bytes=64) for h in range(2)]
+            spread_norms(h, keep.tile([P, HALF], F32, name=f"kn_g{h}"))
         for h in range(2):
-            nc.vector.tensor_copy(scale_g[h][:], scale_table[:].indirect(offsets[:, 32 * h:32 * (h + 1)]))
+            scale_g = keep.tile([P, HALF], U8, name=f"scale_g{h}", align_bytes=64)
+            nc.vector.tensor_copy(scale_g[:], scale_table[:].indirect(offsets[:, 32 * h:32 * (h + 1)]))
             for r in range(4):
-                nc.sync.dma_start(out=scale_plane[h][PLANE_ROW + r:P:32, :].bitcast(I32), in_=scale_g[h][0 + 7 * r:0 + 7 * r + 28 * 3 + 1:28, :].bitcast(I32))
+                nc.sync.dma_start(out=scale_plane[h][PLANE_ROW + r:P:32, :].bitcast(I32),
+                                  in_=scale_g[7 * r:7 * r + 28 * 3 + 1:28, :].bitcast(I32))
 
-        q_codes = keep.tile([P, NQ], U32, name="q_codes", align_bytes=64)
+        q_codes = shared.tile([P, NQ], U32, name="q_codes", align_bytes=64, offset=0)
         q_scales = keep.tile([P, NQ], U8, name="q_scales", align_bytes=64)
         nc.vector.quantize_mx(out=q_codes[:].bitcast(FP8X4), scales=q_scales[:], in_=q_bf[:].rearrange("p q j -> p (q j)"))
 
@@ -101,7 +102,7 @@ def tile_attend_celldist_kernel(tc, qT, k_words, k_scales, kn, qn, offs, out):
         for h in range(2):
             nc.vector.tensor_copy(word_g[h][:], word_table[:].bitcast(U32).indirect(offsets[:, 32 * h:32 * (h + 1)]))
 
-        dots = [psum.tile([P, PIECE], F32, name=f"dots{i}") for i in range(4)]
+        dots = [psum.tile([P, PIECE], F32, name=f"dots{i}", tag=f"dots{i}") for i in range(4)]
         result = keep.tile([P, N // SEG], F32, name="result")
         for i in range(4):
             h, j = divmod(i, 2)
@@ -109,12 +110,15 @@ def tile_attend_celldist_kernel(tc, qT, k_words, k_scales, kn, qn, offs, out):
                                 rhs=word_g[h][:, j * PIECE:(j + 1) * PIECE].bitcast(FP8X4),
                                 rhs_scale=scale_plane[h][PLANE_ROW:P, j * PIECE:(j + 1) * PIECE], start=True, stop=True)
 
+        first_minima = keep.tile([P, HALF // SEG], F32, name="first_minima")
+        minima = [first_minima[:, 0:16], first_minima[:, 16:32], result[:, 32:48], result[:, 48:64]]
         for h in range(2):
             dist = {i: keep.tile([P, PIECE], F32, name=f"dist{i}", tag=f"dist{i % 2}") for i in (2 * h, 2 * h + 1)}
             for i in (2 * h, 2 * h + 1):
                 nc.vector.scalar_tensor_tensor(out=dist[i][:], in0=dots[i][:], scalar=-2.0, in1=norms[i][:],
                                                op0=ALU.mult, op1=ALU.add)
             for i in (2 * h, 2 * h + 1):
-                nc.vector.tensor_reduce(out=result[:, 16 * i:16 * (i + 1)], in_=dist[i][:].rearrange("p (c s) -> p c s", s=SEG),
+                nc.vector.tensor_reduce(out=minima[i], in_=dist[i][:].rearrange("p (c s) -> p c s", s=SEG),
                                         axis=AX.X, op=ALU.min)
+        nc.scalar.activation(out=result[:, 0:HALF // SEG], in_=first_minima[:], func=ACT.Identity, bias=qn_col[:])
         nc.sync.dma_start(out=out[0], in_=result[:])

@@ -29,6 +29,7 @@ BYTES = T * D + 16 * T + 4 * T + 4 * D * NQ + 4 * NQ + 2 * N * 8 + 4 * NQ * (N /
 
 
 PIECE = 256
+GATHERS = ((0, 256), (256, 256), (512, 512))
 
 
 def tile_attend_celldist_kernel(tc, qT, k_words, k_scales, kn, qn, offs, out):
@@ -98,16 +99,18 @@ def tile_attend_celldist_kernel(tc, qT, k_words, k_scales, kn, qn, offs, out):
         q_scales = keep.tile([P, NQ], U8, name="q_scales", align_bytes=64)
         nc.vector.quantize_mx(out=q_codes[:].bitcast(FP8X4), scales=q_scales[:], in_=q_bf[:].rearrange("p q j -> p (q j)"))
 
-        word_g = [keep.tile([P, HALF], U32, name=f"word_g{h}", align_bytes=64) for h in range(2)]
-        for h in range(2):
-            nc.vector.tensor_copy(word_g[h][:], word_table[:].bitcast(U32).indirect(offsets[:, 32 * h:32 * (h + 1)]))
+        word_g = []
+        for first, count in GATHERS:
+            gathered = keep.tile([P, count], U32, name=f"word_g{first}", align_bytes=64)
+            nc.vector.tensor_copy(gathered[:], word_table[:].bitcast(U32).indirect(offsets[:, first // 16:(first + count) // 16]))
+            word_g.extend(gathered[:, c:c + PIECE] for c in range(0, count, PIECE))
 
         dots = [psum.tile([P, PIECE], F32, name=f"dots{i}", tag=f"dots{i}") for i in range(4)]
         result = keep.tile([P, N // SEG], F32, name="result")
         for i in range(4):
             h, j = divmod(i, 2)
             nc.tensor.matmul_mx(out=dots[i][:], lhsT=q_codes[:].bitcast(FP8X4), lhsT_scale=q_scales[:],
-                                rhs=word_g[h][:, j * PIECE:(j + 1) * PIECE].bitcast(FP8X4),
+                                rhs=word_g[i].bitcast(FP8X4),
                                 rhs_scale=scale_plane[h][PLANE_ROW:P, j * PIECE:(j + 1) * PIECE], start=True, stop=True)
 
         first_minima = keep.tile([P, HALF // SEG], F32, name="first_minima")

@@ -22,14 +22,15 @@ D = 512
 SEG = 16
 HALF = 512
 KN_ROW = P - 1
-PLANE_ROW = 4
+ROW_STEP = 8
 
 FLOPS = 2 * NQ * N * D
 BYTES = T * D + 16 * T + 4 * T + 4 * D * NQ + 4 * NQ + 2 * N * 8 + 4 * NQ * (N // SEG)
 
 
 PIECE = 256
-GATHERS = ((0, 256), (256, 256), (512, 512))
+GATHERS = ((0, 256), (256, 256), (512, 256), (768, 256))
+KEYED = 1
 
 
 def tile_attend_celldist_kernel(tc, qT, k_words, k_scales, kn, qn, offs, out):
@@ -55,45 +56,50 @@ def tile_attend_celldist_kernel(tc, qT, k_words, k_scales, kn, qn, offs, out):
         nc.sync.dma_start(out=kn_table[KN_ROW:P, :], in_=kn[0:1, :])
         nc.sync.dma_start(offsets[:], offs)
         nc.scalar.dma_start(out=q_raw[:], in_=qT[0].rearrange("(p j) q -> p j q", j=4))
-        nc.sync.dma_start(out=scale_table[0:0 + 7 * 15 + 1:7, :].bitcast(I32), in_=k_scales[0].bitcast(I32))
+        nc.sync.dma_start(out=scale_table[0:P:ROW_STEP, :].bitcast(I32), in_=k_scales[0].bitcast(I32))
         nc.sync.dma_start(out=word_table[:], in_=words)
         nc.sync.dma_start(out=qn_col[:], in_=qn[0])
         nc.vector.memset(kn_rest, 0)
-        for h in range(2):
-            nc.vector.memset(scale_plane[h][:].bitcast(I32), 0)
         nc.vector.memset(ident[:], 0.0)
         make_identity(nc, ident[:], nomemset=True)
 
         q_bf = keep.tile([P, NQ, 4], BF16, name="q_bf", align_bytes=64)
-        nc.scalar.activation(out=q_bf[:], in_=q_raw[:].rearrange("p j q -> p q j"), func=ACT.Identity)
+        nc.scalar.activation(out=q_bf[:], in_=q_raw[:].rearrange("p j q -> p q j"), func=ACT.Identity, scale=-2.0)
 
-        norms = [keep.tile([P, PIECE], F32, name=f"norms{i}") for i in range(4)]
+        norms = {i: keep.tile([P, PIECE], F32, name=f"norms{i}") for i in range(4) if i != KEYED}
+
+        kn_cols = []
 
         def spread_norms(h, kn_g):
-            nc.vector.tensor_copy(kn_g[:], kn_table[:].indirect(offsets[:, 32 * h:32 * (h + 1)]))
+            listed = kn_table[:].indirect(offsets[:, 32 * h:32 * (h + 1)])
+            if h == 0:
+                nc.vector.tensor_copy(kn_g[:], listed)
+            else:
+                nc.scalar.activation(out=kn_g[:], in_=listed, func=ACT.Copy)
             kn_col = keep.tile([P, 4], F32, name=f"kn_col{h}")
+            kn_cols.append(kn_col)
             for j in range(4):
                 turned = psum.tile([P, P], F32, name=f"turned{h}{j}", tag=f"dots{j}")
                 nc.tensor.transpose(turned[:], kn_g[:, j * P:(j + 1) * P], ident[:])
                 nc.scalar.copy(out=kn_col[:, j:j + 1], in_=turned[:, KN_ROW:P])
             for i in range(2):
+                if 2 * h + i == KEYED:
+                    continue
                 spread = psum.tile([P, 2, P], F32, name=f"spread{h}{i}")
                 for j in range(2):
                     nc.tensor.transpose(spread[:, j, :], kn_col[:, 2 * i + j:2 * i + j + 1].to_broadcast([P, P]), ident[:])
                 flat = spread[:].rearrange("p j s -> p (j s)")
-                if h == 0:
-                    nc.scalar.copy(out=norms[i][:], in_=flat)
-                else:
-                    nc.scalar.activation(out=norms[2 + i][:], in_=flat, func=ACT.Identity, bias=qn_col[:])
+                nc.scalar.copy(out=norms[2 * h + i][:], in_=flat)
 
         for h in range(2):
             spread_norms(h, keep.tile([P, HALF], F32, name=f"kn_g{h}"))
         for h in range(2):
-            scale_g = keep.tile([P, HALF], U8, name=f"scale_g{h}", align_bytes=64)
+            scale_g = keep.tile([P, HALF], U8, name=f"scale_g{h}", tag=f"scale_g{h}", align_bytes=64)
             nc.vector.tensor_copy(scale_g[:], scale_table[:].indirect(offsets[:, 32 * h:32 * (h + 1)]))
-            for r in range(4):
-                nc.sync.dma_start(out=scale_plane[h][PLANE_ROW + r:P:32, :].bitcast(I32),
-                                  in_=scale_g[7 * r:7 * r + 28 * 3 + 1:28, :].bitcast(I32))
+            nc.vector.tensor_copy(scale_plane[h][:].bitcast(I32), scale_g[:].bitcast(I32))
+            for r in range(1, 4):
+                nc.sync.dma_start(out=scale_plane[h][r:P:32, :].bitcast(I32),
+                                  in_=scale_g[ROW_STEP * r:P:32, :].bitcast(I32))
 
         q_codes = shared.tile([P, NQ], U32, name="q_codes", align_bytes=64, offset=0)
         q_scales = keep.tile([P, NQ], U8, name="q_scales", align_bytes=64)
@@ -105,23 +111,56 @@ def tile_attend_celldist_kernel(tc, qT, k_words, k_scales, kn, qn, offs, out):
             nc.vector.tensor_copy(gathered[:], word_table[:].bitcast(U32).indirect(offsets[:, first // 16:(first + count) // 16]))
             word_g.extend(gathered[:, c:c + PIECE] for c in range(0, count, PIECE))
 
-        dots = [psum.tile([P, PIECE], F32, name=f"dots{i}", tag=f"dots{i}") for i in range(4)]
-        result = keep.tile([P, N // SEG], F32, name="result")
+        early = keep.tile([P, 48], F32, name="early")
+        dots = {}
         for i in range(4):
             h, j = divmod(i, 2)
-            nc.tensor.matmul_mx(out=dots[i][:], lhsT=q_codes[:].bitcast(FP8X4), lhsT_scale=q_scales[:],
-                                rhs=word_g[i].bitcast(FP8X4),
-                                rhs_scale=scale_plane[h][PLANE_ROW:P, j * PIECE:(j + 1) * PIECE], start=True, stop=True)
+            plane = scale_plane[h][:, j * PIECE:(j + 1) * PIECE]
+            if i == 0:
+                for b, tag in enumerate(("dots0", "spread00")):
+                    dots[i, b] = psum.tile([P, P], F32, name=f"dots0{b}", tag=tag)
+                    nc.tensor.matmul_mx(out=dots[i, b][:], lhsT=q_codes[:].bitcast(FP8X4), lhsT_scale=q_scales[:],
+                                        rhs=word_g[i][:, b * P:(b + 1) * P].bitcast(FP8X4),
+                                        rhs_scale=plane[:, b * P:(b + 1) * P], start=True, stop=True)
+                continue
+            if i != KEYED:
+                dots[i] = psum.tile([P, PIECE], F32, name=f"dots{i}", tag=f"dots{i}")
+                nc.tensor.matmul_mx(out=dots[i][:], lhsT=q_codes[:].bitcast(FP8X4), lhsT_scale=q_scales[:],
+                                    rhs=word_g[i].bitcast(FP8X4), rhs_scale=plane, start=True, stop=True)
+                continue
+            banks = []
+            for b, tag in enumerate((f"dots{i}", "keyed")):
+                bank = psum.tile([P, NQ], F32, name=f"keyed_dots{b}", tag=tag)
+                nc.tensor.matmul_mx(out=bank[:], lhsT=word_g[i][:, b * P:(b + 1) * P].bitcast(FP8X4),
+                                    lhsT_scale=plane[:, b * P:(b + 1) * P],
+                                    rhs=q_codes[:].bitcast(FP8X4), rhs_scale=q_scales[:], start=True, stop=True)
+                banks.append(bank)
+        by_key = keep.tile([P, 2, NQ], F32, name="by_key", tag="scale_g1", align_bytes=64)
+        for b in range(2):
+            nc.scalar.activation(out=by_key[:, b, :], in_=banks[b][:], func=ACT.Identity,
+                                 bias=kn_cols[0][:, 2 + b:3 + b])
+        back = psum.tile([P, 2, P], F32, name="back", tag="spread10")
+        for b in range(2):
+            nc.tensor.transpose(back[:, b, :], by_key[:, b, :], ident[:])
 
-        first_minima = keep.tile([P, HALF // SEG], F32, name="first_minima")
-        minima = [first_minima[:, 0:16], first_minima[:, 16:32], result[:, 32:48], result[:, 48:64]]
-        for h in range(2):
-            dist = {i: keep.tile([P, PIECE], F32, name=f"dist{i}", tag=f"dist{i % 2}") for i in (2 * h, 2 * h + 1)}
-            for i in (2 * h, 2 * h + 1):
-                nc.vector.scalar_tensor_tensor(out=dist[i][:], in0=dots[i][:], scalar=-2.0, in1=norms[i][:],
-                                               op0=ALU.mult, op1=ALU.add)
-            for i in (2 * h, 2 * h + 1):
-                nc.vector.tensor_reduce(out=minima[i], in_=dist[i][:].rearrange("p (c s) -> p c s", s=SEG),
-                                        axis=AX.X, op=ALU.min)
-        nc.scalar.activation(out=result[:, 0:HALF // SEG], in_=first_minima[:], func=ACT.Identity, bias=qn_col[:])
+        result = keep.tile([P, N // SEG], F32, name="result", tag="scale_g1", align_bytes=64)
+
+        def add(product, addend, name):
+            dist = keep.tile([P, product.shape[1]], F32, name=name)
+            nc.vector.tensor_tensor(out=dist[:], in0=product, in1=addend, op=ALU.add)
+            return dist[:]
+
+        def smallest(dist, into):
+            nc.vector.tensor_reduce(out=into, in_=dist.rearrange("p (c s) -> p c s", s=SEG), axis=AX.X, op=ALU.min)
+
+        first = [add(dots[0, b][:], norms[0][:, b * P:(b + 1) * P], f"dist0{b}") for b in range(2)]
+        for b in range(2):
+            smallest(first[b], early[:, 8 * b:8 * (b + 1)])
+        dist2 = add(dots[2][:], norms[2][:], "dist2")
+        dist3 = keep.tile([P, PIECE], F32, name="dist3")
+        nc.vector.scalar_tensor_tensor(out=dist3[:], in0=dots[3][:], scalar=qn_col[:], in1=norms[3][:], op0=ALU.add, op1=ALU.add)
+        smallest(dist2, early[:, 32:48])
+        smallest(back[:].rearrange("p b s -> p (b s)"), early[:, 16:32])
+        smallest(dist3[:], result[:, 48:64])
+        nc.scalar.activation(out=result[:, 0:48], in_=early[:], func=ACT.Identity, bias=qn_col[:])
         nc.sync.dma_start(out=out[0], in_=result[:])

@@ -30,7 +30,7 @@ BYTES = T * D + 16 * T + 4 * T + 4 * D * NQ + 4 * NQ + 2 * N * 8 + 4 * NQ * (N /
 
 PIECE = 256
 GATHERS = ((0, 256), (256, 256), (512, 256), (768, 256))
-KEYED = 1
+KEYED = 2
 
 
 def tile_attend_celldist_kernel(tc, qT, k_words, k_scales, kn, qn, offs, out):
@@ -94,7 +94,7 @@ def tile_attend_celldist_kernel(tc, qT, k_words, k_scales, kn, qn, offs, out):
         for h in range(2):
             spread_norms(h, keep.tile([P, HALF], F32, name=f"kn_g{h}"))
         for h in range(2):
-            scale_g = keep.tile([P, HALF], U8, name=f"scale_g{h}", tag=f"scale_g{h}", align_bytes=64)
+            scale_g = keep.tile([P, HALF], U8, name=f"scale_g{h}", align_bytes=64)
             nc.vector.tensor_copy(scale_g[:], scale_table[:].indirect(offsets[:, 32 * h:32 * (h + 1)]))
             nc.vector.tensor_copy(scale_plane[h][:].bitcast(I32), scale_g[:].bitcast(I32))
             for r in range(1, 4):
@@ -113,54 +113,47 @@ def tile_attend_celldist_kernel(tc, qT, k_words, k_scales, kn, qn, offs, out):
 
         early = keep.tile([P, 48], F32, name="early")
         dots = {}
+        keyed = []
         for i in range(4):
             h, j = divmod(i, 2)
             plane = scale_plane[h][:, j * PIECE:(j + 1) * PIECE]
-            if i == 0:
-                for b, tag in enumerate(("dots0", "spread00")):
-                    dots[i, b] = psum.tile([P, P], F32, name=f"dots0{b}", tag=tag)
-                    nc.tensor.matmul_mx(out=dots[i, b][:], lhsT=q_codes[:].bitcast(FP8X4), lhsT_scale=q_scales[:],
-                                        rhs=word_g[i][:, b * P:(b + 1) * P].bitcast(FP8X4),
-                                        rhs_scale=plane[:, b * P:(b + 1) * P], start=True, stop=True)
-                continue
             if i != KEYED:
                 dots[i] = psum.tile([P, PIECE], F32, name=f"dots{i}", tag=f"dots{i}")
                 nc.tensor.matmul_mx(out=dots[i][:], lhsT=q_codes[:].bitcast(FP8X4), lhsT_scale=q_scales[:],
                                     rhs=word_g[i].bitcast(FP8X4), rhs_scale=plane, start=True, stop=True)
                 continue
-            banks = []
             for b, tag in enumerate((f"dots{i}", "keyed")):
                 bank = psum.tile([P, NQ], F32, name=f"keyed_dots{b}", tag=tag)
                 nc.tensor.matmul_mx(out=bank[:], lhsT=word_g[i][:, b * P:(b + 1) * P].bitcast(FP8X4),
                                     lhsT_scale=plane[:, b * P:(b + 1) * P],
                                     rhs=q_codes[:].bitcast(FP8X4), rhs_scale=q_scales[:], start=True, stop=True)
-                banks.append(bank)
-        by_key = keep.tile([P, 2, NQ], F32, name="by_key", tag="scale_g1", align_bytes=64)
+                by_key = keep.tile([P, NQ], F32, name=f"by_key{b}", tag=f"by_key{b}")
+                nc.scalar.activation(out=by_key[:], in_=bank[:], func=ACT.Identity,
+                                     bias=kn_cols[h][:, 2 * j + b:2 * j + b + 1])
+                keyed.append(by_key)
+        back = psum.tile([P, 2, P], F32, name="back", tag="spread00")
         for b in range(2):
-            nc.scalar.activation(out=by_key[:, b, :], in_=banks[b][:], func=ACT.Identity,
-                                 bias=kn_cols[0][:, 2 + b:3 + b])
-        back = psum.tile([P, 2, P], F32, name="back", tag="spread10")
-        for b in range(2):
-            nc.tensor.transpose(back[:, b, :], by_key[:, b, :], ident[:])
+            nc.tensor.transpose(back[:, b, :], keyed[b][:], ident[:])
 
-        result = keep.tile([P, N // SEG], F32, name="result", tag="scale_g1", align_bytes=64)
+        result = keep.tile([P, N // SEG], F32, name="result", tag="by_key1")
 
-        def add(product, addend, name):
-            dist = keep.tile([P, product.shape[1]], F32, name=name)
-            nc.vector.tensor_tensor(out=dist[:], in0=product, in1=addend, op=ALU.add)
+        def add(i, tag):
+            dist = keep.tile([P, PIECE], F32, name=f"dist{i}", tag=tag)
+            if i < KEYED:
+                nc.vector.tensor_tensor(out=dist[:], in0=dots[i][:], in1=norms[i][:], op=ALU.add)
+            else:
+                nc.vector.scalar_tensor_tensor(out=dist[:], in0=dots[i][:], scalar=qn_col[:], in1=norms[i][:],
+                                               op0=ALU.add, op1=ALU.add)
             return dist[:]
 
         def smallest(dist, into):
             nc.vector.tensor_reduce(out=into, in_=dist.rearrange("p (c s) -> p c s", s=SEG), axis=AX.X, op=ALU.min)
 
-        first = [add(dots[0, b][:], norms[0][:, b * P:(b + 1) * P], f"dist0{b}") for b in range(2)]
-        for b in range(2):
-            smallest(first[b], early[:, 8 * b:8 * (b + 1)])
-        dist2 = add(dots[2][:], norms[2][:], "dist2")
-        dist3 = keep.tile([P, PIECE], F32, name="dist3")
-        nc.vector.scalar_tensor_tensor(out=dist3[:], in0=dots[3][:], scalar=qn_col[:], in1=norms[3][:], op0=ALU.add, op1=ALU.add)
-        smallest(dist2, early[:, 32:48])
-        smallest(back[:].rearrange("p b s -> p (b s)"), early[:, 16:32])
-        smallest(dist3[:], result[:, 48:64])
+        dist0, dist1 = add(0, "dist0"), add(1, "dist1")
+        smallest(dist0, early[:, 0:16])
+        smallest(dist1, early[:, 16:32])
+        dist3 = add(3, "dist0")
+        smallest(back[:].rearrange("p b s -> p (b s)"), early[:, 32:48])
+        smallest(dist3, result[:, 48:64])
         nc.scalar.activation(out=result[:, 0:48], in_=early[:], func=ACT.Identity, bias=qn_col[:])
         nc.sync.dma_start(out=out[0], in_=result[:])

from contextlib import ExitStack

import concourse.mybir as mybir
from concourse.masks import make_identity

F32 = mybir.dt.float32
BF16 = mybir.dt.bfloat16
I32 = mybir.dt.int32
U32 = mybir.dt.uint32
U16 = mybir.dt.uint16
U8 = mybir.dt.uint8
FP8X4 = mybir.dt.float8_e4m3fn_x4
ALU = mybir.AluOpType
ACT = mybir.ActivationFunctionType
AX = mybir.AxisListType

P = 128
T = 4096
N = 1024
NQ = 128
D = 512
SEG = 16
HALF = 512
KN_ROW = P - 1
ROW_STEP = 8

FLOPS = 2 * NQ * N * D
BYTES = T * D + 16 * T + 4 * T + 4 * D * NQ + 4 * NQ + 2 * N * 8 + 4 * NQ * (N // SEG)


PIECE = 256
GATHERS = ((0, 256), (256, 256), (512, 256), (768, 256))
KEYED = 2


def tile_attend_celldist_kernel(tc, qT, k_words, k_scales, kn, qn, offs, out):
    nc = tc.nc
    with ExitStack() as ctx:
        keep = ctx.enter_context(tc.tile_pool(name="keep", bufs=1))
        shared = ctx.enter_context(tc.tile_pool(name="shared", bufs=1))
        psum = ctx.enter_context(tc.psum_pool(name="psum", bufs=1))

        offsets = keep.tile([P, N // 16], U16, name="offsets")
        scale_table = shared.tile([P, T], U8, name="scale_table", align_bytes=64, offset=0)
        kn_table = keep.tile([P, T], F32, name="kn_table")
        word_table = keep.tile([P, T], I32, name="word_table")
        q_raw = keep.tile([P, 4, NQ], F32, name="q_raw")
        qn_col = keep.tile([P, 1], F32, name="qn_col")
        scale_plane = [keep.tile([P, HALF], U8, name=f"scale_plane{h}", align_bytes=64) for h in range(2)]
        ident = keep.tile([P, P], F32, name="ident")
        words = k_words[0].rearrange("p n t -> p (n t)").bitcast(I32)

        scale_words = scale_table[:].bitcast(I32)
        kn_rest = kn_table[0:KN_ROW, :].bitcast(I32)
        nc.vector.memset(scale_words, 0)
        nc.sync.dma_start(out=kn_table[KN_ROW:P, :], in_=kn[0:1, :])
        nc.sync.dma_start(offsets[:], offs)
        nc.scalar.dma_start(out=q_raw[:], in_=qT[0].rearrange("(p j) q -> p j q", j=4))
        nc.sync.dma_start(out=scale_table[0:P:ROW_STEP, :].bitcast(I32), in_=k_scales[0].bitcast(I32))
        nc.sync.dma_start(out=word_table[:], in_=words)
        nc.sync.dma_start(out=qn_col[:], in_=qn[0])
        nc.vector.memset(kn_rest, 0)
        nc.vector.memset(ident[:], 0.0)
        make_identity(nc, ident[:], nomemset=True)

        q_bf = keep.tile([P, NQ, 4], BF16, name="q_bf", align_bytes=64)
        nc.scalar.activation(out=q_bf[:], in_=q_raw[:].rearrange("p j q -> p q j"), func=ACT.Identity, scale=-2.0)

        norms = {i: keep.tile([P, PIECE], F32, name=f"norms{i}") for i in range(4) if i != KEYED}

        kn_cols = []

        def spread_norms(h, kn_g):
            listed = kn_table[:].indirect(offsets[:, 32 * h:32 * (h + 1)])
            if h == 0:
                nc.vector.tensor_copy(kn_g[:], listed)
            else:
                nc.scalar.activation(out=kn_g[:], in_=listed, func=ACT.Copy)
            kn_col = keep.tile([P, 4], F32, name=f"kn_col{h}")
            kn_cols.append(kn_col)
            for j in range(4):
                turned = psum.tile([P, P], F32, name=f"turned{h}{j}", tag=f"dots{j}")
                nc.tensor.transpose(turned[:], kn_g[:, j * P:(j + 1) * P], ident[:])
                nc.scalar.copy(out=kn_col[:, j:j + 1], in_=turned[:, KN_ROW:P])
            for i in range(2):
                if 2 * h + i == KEYED:
                    continue
                spread = psum.tile([P, 2, P], F32, name=f"spread{h}{i}")
                for j in range(2):
                    nc.tensor.transpose(spread[:, j, :], kn_col[:, 2 * i + j:2 * i + j + 1].to_broadcast([P, P]), ident[:])
                flat = spread[:].rearrange("p j s -> p (j s)")
                nc.scalar.copy(out=norms[2 * h + i][:], in_=flat)

        for h in range(2):
            spread_norms(h, keep.tile([P, HALF], F32, name=f"kn_g{h}"))
        for h in range(2):
            scale_g = keep.tile([P, HALF], U8, name=f"scale_g{h}", align_bytes=64)
            nc.vector.tensor_copy(scale_g[:], scale_table[:].indirect(offsets[:, 32 * h:32 * (h + 1)]))
            nc.vector.tensor_copy(scale_plane[h][:].bitcast(I32), scale_g[:].bitcast(I32))
            for r in range(1, 4):
                nc.sync.dma_start(out=scale_plane[h][r:P:32, :].bitcast(I32),
                                  in_=scale_g[ROW_STEP * r:P:32, :].bitcast(I32))

        q_codes = shared.tile([P, NQ], U32, name="q_codes", align_bytes=64, offset=0)
        q_scales = keep.tile([P, NQ], U8, name="q_scales", align_bytes=64)
        nc.vector.quantize_mx(out=q_codes[:].bitcast(FP8X4), scales=q_scales[:], in_=q_bf[:].rearrange("p q j -> p (q j)"))

        word_g = []
        for first, count in GATHERS:
            gathered = keep.tile([P, count], U32, name=f"word_g{first}", align_bytes=64)
            nc.vector.tensor_copy(gathered[:], word_table[:].bitcast(U32).indirect(offsets[:, first // 16:(first + count) // 16]))
            word_g.extend(gathered[:, c:c + PIECE] for c in range(0, count, PIECE))

        early = keep.tile([P, 48], F32, name="early")
        dots = {}
        keyed = []
        for i in range(4):
            h, j = divmod(i, 2)
            plane = scale_plane[h][:, j * PIECE:(j + 1) * PIECE]
            if i != KEYED:
                dots[i] = psum.tile([P, PIECE], F32, name=f"dots{i}", tag=f"dots{i}")
                nc.tensor.matmul_mx(out=dots[i][:], lhsT=q_codes[:].bitcast(FP8X4), lhsT_scale=q_scales[:],
                                    rhs=word_g[i].bitcast(FP8X4), rhs_scale=plane, start=True, stop=True)
                continue
            for b, tag in enumerate((f"dots{i}", "keyed")):
                bank = psum.tile([P, NQ], F32, name=f"keyed_dots{b}", tag=tag)
                nc.tensor.matmul_mx(out=bank[:], lhsT=word_g[i][:, b * P:(b + 1) * P].bitcast(FP8X4),
                                    lhsT_scale=plane[:, b * P:(b + 1) * P],
                                    rhs=q_codes[:].bitcast(FP8X4), rhs_scale=q_scales[:], start=True, stop=True)
                by_key = keep.tile([P, NQ], F32, name=f"by_key{b}", tag=f"by_key{b}")
                nc.scalar.activation(out=by_key[:], in_=bank[:], func=ACT.Identity,
                                     bias=kn_cols[h][:, 2 * j + b:2 * j + b + 1])
                keyed.append(by_key)
        back = psum.tile([P, 2, P], F32, name="back", tag="spread00")
        for b in range(2):
            nc.tensor.transpose(back[:, b, :], keyed[b][:], ident[:])

        result = keep.tile([P, N // SEG], F32, name="result", tag="by_key1")

        def add(i, tag):
            dist = keep.tile([P, PIECE], F32, name=f"dist{i}", tag=tag)
            if i < KEYED:
                nc.vector.tensor_tensor(out=dist[:], in0=dots[i][:], in1=norms[i][:], op=ALU.add)
            else:
                nc.vector.scalar_tensor_tensor(out=dist[:], in0=dots[i][:], scalar=qn_col[:], in1=norms[i][:],
                                               op0=ALU.add, op1=ALU.add)
            return dist[:]

        def smallest(dist, into):
            nc.vector.tensor_reduce(out=into, in_=dist.rearrange("p (c s) -> p c s", s=SEG), axis=AX.X, op=ALU.min)

        dist0, dist1 = add(0, "dist0"), add(1, "dist1")
        smallest(dist0, early[:, 0:16])
        smallest(dist1, early[:, 16:32])
        dist3 = add(3, "dist0")
        smallest(back[:].rearrange("p b s -> p (b s)"), early[:, 32:48])
        smallest(dist3, result[:, 48:64])
        nc.scalar.activation(out=result[:, 0:48], in_=early[:], func=ACT.Identity, bias=qn_col[:])
        nc.sync.dma_start(out=out[0], in_=result[:])
